import numpy as np
import ml_dtypes


def mxq(x, axis, fmt="e4m3"):
    dtype, down = {"e4m3": (ml_dtypes.float8_e4m3fn, 7), "e5m2": (ml_dtypes.float8_e5m2, 14)}[fmt]
    v = np.moveaxis(np.asarray(x, np.float32).astype(ml_dtypes.bfloat16).astype(np.float64), axis, -1)
    blocks = v.reshape(v.shape[:-1] + (-1, 32))
    amax = np.abs(blocks).max(-1, keepdims=True)
    byte = np.maximum(np.where(amax > 0, np.frexp(amax)[1] - 1 + 127, 0) - down, 1)
    scale = np.exp2(byte - 127.0)
    codes = (blocks / scale).astype(np.float32).astype(dtype).astype(np.float64)
    return np.moveaxis((codes * scale).reshape(v.shape), -1, axis)


WIDE = False


def mx_kscale(k):
    if not WIDE:
        return np.ones(k)
    levels = np.array([10, -10, 5, -5, 0])
    if k % 512:
        return np.exp2(np.random.permutation(np.resize(levels, k // 32))).repeat(32)
    a = np.empty((k // 512, 16))
    for p in range(k // 512):
        a[p, :8] = np.random.permutation(np.resize(levels, 8))
        for g in range(8):
            far = levels[np.abs(levels - a[p, g]) >= 10]
            a[p, g + 8] = far[np.random.randint(len(far))]
    return np.exp2(a.ravel()).repeat(32)


def f64(x):
    return np.asarray(x).astype(np.float64)


def striped(idx):
    return np.tile(idx.reshape(-1, 16).T, (8, 1)).astype(np.uint16)


def unstriped(offs):
    return offs[:16].T.reshape(-1).astype(np.int64)


def pack_weight(w):
    k, n = w.shape
    w = f64(np.asarray(w, np.float32).astype(ml_dtypes.bfloat16)).reshape(k // 32, 32, n)
    amax = np.abs(w).max(1)
    byte = np.clip(np.where(amax > 0, np.frexp(amax)[1] - 1 + 127 - 7, 1), 1, 254)
    scaled = (w * np.exp2(127.0 - byte)[:, None, :]).reshape(k, n).astype(np.float32)
    words = np.ascontiguousarray(scaled.reshape(k // 512, 128, 4, n).transpose(0, 1, 3, 2)).astype(ml_dtypes.float8_e4m3fn).view(np.uint8)
    return words, np.ascontiguousarray(byte.astype(np.uint8).reshape(k // 512, 16, n))


def unpack_weight(words, scales):
    g, p, n, _ = words.shape
    vals = np.ascontiguousarray(words).view(ml_dtypes.float8_e4m3fn).astype(np.float64) * np.repeat(np.exp2(scales.astype(np.float64) - 127.0), 8, axis=1)[..., None]
    return vals.transpose(0, 1, 3, 2).reshape(g * 512, n)


def sigmoid(v):
    return 1.0 / (1.0 + np.exp(-np.maximum(v, -700.0)))


K, T, S, H, N, U = 1024, 2048, 512, 512, 256, 1024
P = 2 ** 7


def setup_inputs():
    n = np.random.standard_normal
    s = mx_kscale(K)[:, None]
    u = mx_kscale(H)
    packed_xT = pack_weight(n((K, T)) * s)
    return {
        "x_words": packed_xT[0],
        "x_scales": packed_xT[1],
        "w1": (n((K, H)) / np.sqrt(K) / s).astype(np.float32),
        "gap": (np.tile(np.random.uniform(0.1, 2.0, S), (P, 1))).astype(np.float32),
        "base": (np.random.uniform(0.1, 0.5, (H, 1))).astype(np.float32),
        "rf": (-np.random.uniform(0.3, 2.0, (H, 1))).astype(np.float32),
        "rd": (-np.random.uniform(0.3, 2.0, (H, 1))).astype(np.float32),
        "use": (np.random.uniform(-0.1, 0.4, (H, U))).astype(np.float32),
        "gone": (np.random.uniform(0.0, 0.8, (H, U))).astype(np.float32),
        "w2": (n((H, N)) / np.sqrt(H) / u[:, None]).astype(np.float32),
        "unit": (np.random.uniform(0.5, 1.5, (H, 1)) * u[:, None]).astype(np.float32),
        "offs": striped(np.random.permutation(T)[:S]),
        "slot": striped(np.random.permutation(U)[:S]),
    }


def reference(x_words, x_scales, w1, gap, base, rf, rd, use, gone, w2, unit, offs, slot):
    fu = np.exp(f64(rf) * f64(gap)[:1])
    u0 = f64(use)[:, unstriped(slot)] * fu + f64(base)
    xq = unpack_weight(x_words, x_scales)[:, unstriped(offs)]
    ss = sigmoid(mxq(f64(w1), 0, "e4m3").T @ xq)
    u1 = u0 + f64(base) * (ss - (ss * u0))
    fd = np.exp(f64(rd) * f64(gap)[:1])
    x0 = -1.0 * (f64(gone)[:, unstriped(slot)] * fd) + 1.0
    rel = (u1 * x0) * ss
    z = f64(unit) * rel
    return mxq(f64(w2), 0, "e4m3").T @ mxq(z, 0, "e4m3")

@@ -1,0 +1,218 @@
+from contextlib import ExitStack
+
+import concourse.mybir as mybir
+
+K, T, S, H, N, U = 1024, 2048, 512, 512, 256, 1024
+FLOPS = 2 * K * H * S + 2 * H * N * S
+
+F32 = mybir.dt.float32
+BF16 = mybir.dt.bfloat16
+I32 = mybir.dt.int32
+U32 = mybir.dt.uint32
+U16 = mybir.dt.uint16
+U8 = mybir.dt.uint8
+FP8X4 = mybir.dt.float8_e4m3fn_x4
+ACT = mybir.ActivationFunctionType
+ALU = mybir.AluOpType
+
+P = 128
+PACK = 4
+PASSES = K // (P * PACK)
+LANES = 16
+CHUNKS = ((0, 256), (256, 384), (384, 512))
+
+
+def tile_picked_ystp_cur_p_kernel(tc, x_words, x_scales, w1, gap, base, rf, rd, use, gone, w2, unit, offs, slot, out):
+    nc = tc.nc
+    with ExitStack() as ctx:
+        keep = ctx.enter_context(tc.tile_pool(name="keep", bufs=1))
+        psum = ctx.enter_context(tc.psum_pool(name="psum", bufs=1))
+
+        def per_row(name, vector, queue):
+            tile = keep.tile([P, PACK], F32, name=name)
+            queue.dma_start(out=tile[:], in_=vector.rearrange("(p t) o -> p (t o)", t=PACK))
+            return tile
+
+        scale_window = keep.tile([P, T], U8, name="scale_window", align_bytes=64)
+        nc.gpsimd.memset(scale_window[:].bitcast(I32), 0)
+        for q in range(4):
+            nc.gpsimd.dma_start(
+                out=scale_window[32 * q : 32 * q + 4 * PASSES, :].bitcast(I32),
+                in_=x_scales[:, 4 * q : 4 * q + 4, :].bitcast(I32),
+            )
+        base_sb = per_row("base_sb", base, nc.gpsimd)
+        unit_sb = per_row("unit_sb", unit, nc.gpsimd)
+
+        gap_sb = keep.tile([P, S], F32, name="gap_sb")
+        nc.scalar.dma_start(out=gap_sb[:], in_=gap)
+        rf_sb = per_row("rf_sb", rf, nc.scalar)
+        rd_sb = per_row("rd_sb", rd, nc.scalar)
+
+        w1_raw = [keep.tile([P, PACK, H], F32, name=f"w1_raw{o}") for o in range(PASSES)]
+        word_window = [keep.tile([P, T], U32, name=f"word_window{o}", align_bytes=64) for o in range(PASSES)]
+        offs_sb = keep.tile([P, S // LANES], U16, name="offs_sb")
+        slot_sb = keep.tile([P, S // LANES], U16, name="slot_sb")
+        use_rows = [keep.tile([P, U], F32, name=f"use_rows{t}") for t in range(PACK)]
+        gone_rows = [keep.tile([P, U], F32, name=f"gone_rows{t}") for t in range(PACK)]
+        w2_raw = keep.tile([P, PACK, N], F32, name="w2_raw")
+
+        for o in range(PASSES):
+            nc.sync.dma_start(out=w1_raw[o][:], in_=w1[512 * o : 512 * (o + 1), :].rearrange("(p j) c -> p j c", j=PACK))
+        nc.sync.dma_start(offs_sb[:], offs)
+        for o in range(PASSES):
+            nc.sync.dma_start(
+                out=word_window[o][:].bitcast(I32),
+                in_=x_words[o].rearrange("p n t -> p (n t)").bitcast(I32),
+            )
+        nc.sync.dma_start(slot_sb[:], slot)
+        use_dealt = use.rearrange("(p t) u -> t p u", t=PACK)
+        gone_dealt = gone.rearrange("(p t) u -> t p u", t=PACK)
+        for t in range(PACK):
+            nc.sync.dma_start(out=use_rows[t][:], in_=use_dealt[t])
+            nc.sync.dma_start(out=gone_rows[t][:], in_=gone_dealt[t])
+            if t == 1:
+                nc.sync.dma_start(out=w2_raw[:], in_=w2.rearrange("(p j) c -> p j c", j=PACK))
+
+        base_less_one = keep.tile([P, PACK], F32, name="base_less_one")
+        unit_base = keep.tile([P, PACK], F32, name="unit_base")
+        minus_unit = keep.tile([P, PACK], F32, name="minus_unit")
+        nc.gpsimd.tensor_scalar(base_less_one[:], base_sb[:], 1.0, -1.0, ALU.mult, ALU.add)
+        nc.gpsimd.tensor_tensor(unit_base[:], unit_sb[:], base_sb[:], ALU.mult)
+        nc.gpsimd.tensor_scalar(minus_unit[:], unit_sb[:], -1.0, 0.0, ALU.mult, ALU.add)
+
+        fu = [keep.tile([P, S], F32, name=f"fu{t}") for t in range(PACK)]
+        fd = [keep.tile([P, S], F32, name=f"fd{t}") for t in range(PACK)]
+        for t in range(PACK):
+            nc.scalar.activation(fu[t][:], gap_sb[:], ACT.Exp, scale=rf_sb[:, t : t + 1])
+            nc.scalar.activation(fd[t][:], gap_sb[:], ACT.Exp, scale=rd_sb[:, t : t + 1])
+
+        w1_codes = [keep.tile([P, H], U32, name=f"w1_codes{o}", align_bytes=64) for o in range(PASSES)]
+        w1_scales = [keep.tile([P, H], U8, name=f"w1_scales{o}", align_bytes=64) for o in range(PASSES)]
+        w1_grouped = [keep.tile([P, H * PACK], BF16, name=f"w1_grouped{o}", align_bytes=64) for o in range(PASSES)]
+        for o in range(PASSES):
+            nc.vector.tensor_copy(
+                out=w1_grouped[o][:].rearrange("p (t m j) -> p m j t", t=PACK, j=PACK),
+                in_=w1_raw[o][:].rearrange("p j (m t) -> p m j t", t=PACK),
+            )
+            nc.vector.quantize_mx(out=w1_codes[o][:].bitcast(FP8X4), scales=w1_scales[o][:], in_=w1_grouped[o][:])
+
+        x_scale = keep.tile([P, S], U8, name="x_scale", align_bytes=64)
+        nc.vector.tensor_copy(x_scale[:], scale_window[:].indirect(offs_sb[:]))
+        x_codes = [keep.tile([P, S], U32, name=f"x_codes{o}", align_bytes=64) for o in range(PASSES)]
+        for o in range(PASSES):
+            nc.vector.tensor_copy(x_codes[o][:], word_window[o][:].indirect(offs_sb[:]))
+
+        drive = [psum.tile([P, S], F32, name=f"drive{t}") for t in range(PACK)]
+        for o in range(PASSES):
+            for t in range(PACK):
+                cols = slice(P * t, P * (t + 1))
+                nc.tensor.matmul_mx(
+                    out=drive[t][:],
+                    lhsT=w1_codes[o][:, cols].bitcast(FP8X4),
+                    lhsT_scale=w1_scales[o][:, cols],
+                    rhs=x_codes[o][:].bitcast(FP8X4),
+                    rhs_scale=x_scale[4 * o :, :],
+                    start=(o == 0),
+                    stop=(o == PASSES - 1),
+                )
+
+        ss = [keep.tile([P, S], F32, name=f"ss{t}") for t in range(PACK)]
+        keepfrac = [keep.tile([P, S], F32, name=f"keepfrac{t}") for t in range(PACK)]
+        for t in range(PACK):
+            nc.scalar.activation(ss[t][:], drive[t][:], ACT.Sigmoid)
+            nc.scalar.activation(
+                keepfrac[t][:], ss[t][:], ACT.Identity, scale=unit_base[:, t : t + 1], bias=minus_unit[:, t : t + 1]
+            )
+
+        w2_grouped = keep.tile([P, N, PACK], BF16, name="w2_grouped", align_bytes=64)
+        w2_codes = keep.tile([P, N], U32, name="w2_codes", align_bytes=64)
+        w2_scales = keep.tile([P, N], U8, name="w2_scales", align_bytes=64)
+        nc.scalar.copy(
+            out=w2_grouped[:].rearrange("p (c i) j -> p c j i", i=4),
+            in_=w2_raw[:].rearrange("p j (c i) -> p c j i", i=4),
+        )
+
+        a = [keep.tile([P, S], F32, name=f"a{t}") for t in range(PACK)]
+        g = [keep.tile([P, S], F32, name=f"g{t}") for t in range(PACK)]
+        unused = [keep.tile([P, S], F32, name=f"unused{t}") for t in range(PACK)]
+        left = [keep.tile([P, S], F32, name=f"left{t}") for t in range(PACK)]
+        z = keep.tile([P, PACK, S], BF16, name="z")
+
+        def gather_use(t, lo, hi):
+            picks = slot_sb[:, lo // LANES : hi // LANES]
+            nc.vector.tensor_tensor(a[t][:, lo:hi], use_rows[t][:].indirect(picks), fu[t][:, lo:hi], ALU.mult)
+
+        def gather_gone(t, lo, hi):
+            picks = slot_sb[:, lo // LANES : hi // LANES]
+            nc.vector.tensor_tensor(g[t][:, lo:hi], gone_rows[t][:].indirect(picks), fd[t][:, lo:hi], ALU.mult)
+
+        def make_unused(t, lo, hi):
+            nc.vector.scalar_tensor_tensor(
+                unused[t][:, lo:hi], a[t][:, lo:hi], base_less_one[:, t : t + 1], keepfrac[t][:, lo:hi], ALU.add, ALU.mult
+            )
+
+        def make_left(t, lo, hi):
+            nc.vector.scalar_tensor_tensor(left[t][:, lo:hi], g[t][:, lo:hi], 1.0, ss[t][:, lo:hi], ALU.subtract, ALU.mult)
+
+        def make_z(t, lo, hi):
+            nc.vector.scalar_tensor_tensor(
+                z[:, t, lo:hi], unused[t][:, lo:hi], unit_sb[:, t : t + 1], left[t][:, lo:hi], ALU.subtract, ALU.mult
+            )
+
+        out_dealt = out.rearrange("(m p) j -> p m j", p=P)
+
+        def interleave(c):
+            lo, hi = CHUNKS[c]
+            z_grouped = keep.tile([P, hi - lo, PACK], BF16, name=f"z_grouped{c}", align_bytes=64)
+            nc.scalar.copy(
+                out=z_grouped[:].rearrange("p (c i) t -> p c t i", i=4),
+                in_=z[:, :, lo:hi].rearrange("p t (c i) -> p c t i", i=4),
+            )
+            return z_grouped
+
+        def finish(c, z_grouped):
+            lo, hi = CHUNKS[c]
+            z_codes = keep.tile([P, hi - lo], U32, name=f"z_codes{c}", align_bytes=64)
+            z_scales = keep.tile([P, hi - lo], U8, name=f"z_scales{c}", align_bytes=64)
+            nc.vector.quantize_mx(
+                out=z_codes[:].bitcast(FP8X4), scales=z_scales[:], in_=z_grouped[:].rearrange("p c t -> p (c t)")
+            )
+            current = psum.tile([P, N // P, hi - lo], F32, name=f"current{c}")
+            for m in range(N // P):
+                cols = slice(P * m, P * (m + 1))
+                nc.tensor.matmul_mx(
+                    out=current[:, m, :],
+                    lhsT=w2_codes[:, cols].bitcast(FP8X4),
+                    lhsT_scale=w2_scales[:, cols],
+                    rhs=z_codes[:].bitcast(FP8X4),
+                    rhs_scale=z_scales[:],
+                    start=True,
+                    stop=True,
+                )
+            result = keep.tile([P, N // P, hi - lo], F32, name=f"result{c}")
+            nc.scalar.copy(out=result[:], in_=current[:])
+            nc.sync.dma_start(out=out_dealt[:, :, lo:hi], in_=result[:])
+
+        gather_use(0, 0, S)
+        gather_gone(0, 0, S)
+        make_unused(0, 0, S)
+        make_left(0, 0, S)
+        gather_use(1, 0, S)
+        make_z(0, 0, S)
+        gather_gone(1, 0, S)
+        make_unused(1, 0, S)
+        make_left(1, 0, S)
+        nc.vector.quantize_mx(
+            out=w2_codes[:].bitcast(FP8X4), scales=w2_scales[:], in_=w2_grouped[:].rearrange("p c j -> p (c j)")
+        )
+        make_z(1, 0, S)
+        pending = None
+        for c in range(len(CHUNKS)):
+            lo, hi = CHUNKS[c]
+            for step in (gather_use, gather_gone, make_unused, make_left, make_z):
+                for t in (2, 3):
+                    step(t, lo, hi)
+                if step is make_unused and pending is not None:
+                    finish(c - 1, pending)
+            pending = interleave(c)
+        finish(len(CHUNKS) - 1, pending)

@@ -1,6 +1,7 @@
 from contextlib import ExitStack
 
 import concourse.mybir as mybir
+from concourse.masks import make_identity
 
 K, T, S, H, N, U = 1024, 2048, 512, 512, 256, 1024
 FLOPS = 2 * K * H * S + 2 * H * N * S
@@ -34,17 +35,19 @@ def tile_picked_ystp_cur_p_kernel(tc, x_words, x_scales, w1, gap, base, rf, rd, 
             return tile
 
         scale_window = keep.tile([P, T], U8, name="scale_window", align_bytes=64)
-        nc.gpsimd.memset(scale_window[:].bitcast(I32), 0)
+        nc.vector.memset(scale_window[:].bitcast(I32), 0)
+        identity = keep.tile([P, P], F32, name="identity")
+        make_identity(nc, identity[:])
+        unit_sb = per_row("unit_sb", unit, nc.gpsimd)
+        base_sb = per_row("base_sb", base, nc.gpsimd)
+
+        gap_col = keep.tile([P, PACK], F32, name="gap_col")
+        nc.sync.dma_start(out=gap_col[:], in_=gap[0].rearrange("(p c) -> p c", c=PACK))
         for q in range(4):
-            nc.gpsimd.dma_start(
+            nc.sync.dma_start(
                 out=scale_window[32 * q : 32 * q + 4 * PASSES, :].bitcast(I32),
                 in_=x_scales[:, 4 * q : 4 * q + 4, :].bitcast(I32),
             )
-        base_sb = per_row("base_sb", base, nc.gpsimd)
-        unit_sb = per_row("unit_sb", unit, nc.gpsimd)
-
-        gap_sb = keep.tile([P, S], F32, name="gap_sb")
-        nc.scalar.dma_start(out=gap_sb[:], in_=gap)
         rf_sb = per_row("rf_sb", rf, nc.scalar)
         rd_sb = per_row("rd_sb", rd, nc.scalar)
 
@@ -74,17 +77,24 @@ def tile_picked_ystp_cur_p_kernel(tc, x_words, x_scales, w1, gap, base, rf, rd, 
                 nc.sync.dma_start(out=w2_raw[:], in_=w2.rearrange("(p j) c -> p j c", j=PACK))
 
         base_less_one = keep.tile([P, PACK], F32, name="base_less_one")
-        unit_base = keep.tile([P, PACK], F32, name="unit_base")
-        minus_unit = keep.tile([P, PACK], F32, name="minus_unit")
         nc.gpsimd.tensor_scalar(base_less_one[:], base_sb[:], 1.0, -1.0, ALU.mult, ALU.add)
-        nc.gpsimd.tensor_tensor(unit_base[:], unit_sb[:], base_sb[:], ALU.mult)
-        nc.gpsimd.tensor_scalar(minus_unit[:], unit_sb[:], -1.0, 0.0, ALU.mult, ALU.add)
 
         fu = [keep.tile([P, S], F32, name=f"fu{t}") for t in range(PACK)]
         fd = [keep.tile([P, S], F32, name=f"fd{t}") for t in range(PACK)]
+        fd_unit = [keep.tile([P, S], F32, name=f"fd_unit{t}") for t in range(PACK)]
+        gap_ps = psum.tile([P, PACK, P], F32, name="gap_ps")
+        for c in range(PACK):
+            nc.tensor.transpose(gap_ps[:, c, :], gap_col[:, c : c + 1].to_broadcast([P, P]), identity[:])
+        gap_rows = gap_ps[:].rearrange("p c n -> p n c")
         for t in range(PACK):
-            nc.scalar.activation(fu[t][:], gap_sb[:], ACT.Exp, scale=rf_sb[:, t : t + 1])
-            nc.scalar.activation(fd[t][:], gap_sb[:], ACT.Exp, scale=rd_sb[:, t : t + 1])
+            nc.scalar.activation(
+                fu[t][:].rearrange("p (n c) -> p n c", c=PACK), gap_rows, ACT.Exp, scale=rf_sb[:, t : t + 1]
+            )
+            nc.scalar.activation(
+                fd[t][:].rearrange("p (n c) -> p n c", c=PACK), gap_rows, ACT.Exp, scale=rd_sb[:, t : t + 1]
+            )
+        for t in range(PACK):
+            nc.scalar.activation(fd_unit[t][:], fd[t][:], ACT.Copy, scale=unit_sb[:, t : t + 1])
 
         w1_codes = [keep.tile([P, H], U32, name=f"w1_codes{o}", align_bytes=64) for o in range(PASSES)]
         w1_scales = [keep.tile([P, H], U8, name=f"w1_scales{o}", align_bytes=64) for o in range(PASSES)]
@@ -121,7 +131,7 @@ def tile_picked_ystp_cur_p_kernel(tc, x_words, x_scales, w1, gap, base, rf, rd, 
         for t in range(PACK):
             nc.scalar.activation(ss[t][:], drive[t][:], ACT.Sigmoid)
             nc.scalar.activation(
-                keepfrac[t][:], ss[t][:], ACT.Identity, scale=unit_base[:, t : t + 1], bias=minus_unit[:, t : t + 1]
+                keepfrac[t][:], ss[t][:], ACT.Copy, scale=base_sb[:, t : t + 1], bias=-1.0
             )
 
         w2_grouped = keep.tile([P, N, PACK], BF16, name="w2_grouped", align_bytes=64)
@@ -134,9 +144,9 @@ def tile_picked_ystp_cur_p_kernel(tc, x_words, x_scales, w1, gap, base, rf, rd, 
 
         a = [keep.tile([P, S], F32, name=f"a{t}") for t in range(PACK)]
         g = [keep.tile([P, S], F32, name=f"g{t}") for t in range(PACK)]
-        unused = [keep.tile([P, S], F32, name=f"unused{t}") for t in range(PACK)]
-        left = [keep.tile([P, S], F32, name=f"left{t}") for t in range(PACK)]
-        z = keep.tile([P, PACK, S], BF16, name="z")
+        unused = keep.tile([P, PACK, S], F32, name="unused")
+        left = keep.tile([P, PACK, S], F32, name="left")
+        z = keep.tile([P, PACK, CHUNKS[-1][0]], BF16, name="z")
 
         def gather_use(t, lo, hi):
             picks = slot_sb[:, lo // LANES : hi // LANES]
@@ -144,19 +154,34 @@ def tile_picked_ystp_cur_p_kernel(tc, x_words, x_scales, w1, gap, base, rf, rd, 
 
         def gather_gone(t, lo, hi):
             picks = slot_sb[:, lo // LANES : hi // LANES]
-            nc.vector.tensor_tensor(g[t][:, lo:hi], gone_rows[t][:].indirect(picks), fd[t][:, lo:hi], ALU.mult)
+            nc.vector.tensor_tensor(g[t][:, lo:hi], gone_rows[t][:].indirect(picks), fd_unit[t][:, lo:hi], ALU.mult)
 
         def make_unused(t, lo, hi):
             nc.vector.scalar_tensor_tensor(
-                unused[t][:, lo:hi], a[t][:, lo:hi], base_less_one[:, t : t + 1], keepfrac[t][:, lo:hi], ALU.add, ALU.mult
+                unused[:, t, lo:hi], a[t][:, lo:hi], base_less_one[:, t : t + 1], keepfrac[t][:, lo:hi], ALU.add, ALU.mult
             )
 
         def make_left(t, lo, hi):
-            nc.vector.scalar_tensor_tensor(left[t][:, lo:hi], g[t][:, lo:hi], 1.0, ss[t][:, lo:hi], ALU.subtract, ALU.mult)
+            nc.vector.scalar_tensor_tensor(
+                left[:, t, lo:hi], g[t][:, lo:hi], unit_sb[:, t : t + 1], ss[t][:, lo:hi], ALU.subtract, ALU.mult
+            )
 
         def make_z(t, lo, hi):
             nc.vector.scalar_tensor_tensor(
-                z[:, t, lo:hi], unused[t][:, lo:hi], unit_sb[:, t : t + 1], left[t][:, lo:hi], ALU.subtract, ALU.mult
+                z[:, t, lo:hi], unused[:, t, lo:hi], 1.0, left[:, t, lo:hi], ALU.subtract, ALU.mult
+            )
+
+        last_lo = CHUNKS[-1][0]
+        last_grouped = keep.tile([P, S - last_lo, PACK], BF16, name="last_grouped", align_bytes=64)
+
+        def make_last_pair(t):
+            nc.vector.scalar_tensor_tensor(
+                last_grouped[:, :, t : t + 2],
+                unused[:, t : t + 2, last_lo:].rearrange("p t j -> p j t"),
+                1.0,
+                left[:, t : t + 2, last_lo:].rearrange("p t j -> p j t"),
+                ALU.subtract,
+                ALU.mult,
             )
 
         out_dealt = out.rearrange("(m p) j -> p m j", p=P)
@@ -198,21 +223,26 @@ def tile_picked_ystp_cur_p_kernel(tc, x_words, x_scales, w1, gap, base, rf, rd, 
         make_unused(0, 0, S)
         make_left(0, 0, S)
         gather_use(1, 0, S)
-        make_z(0, 0, S)
+        make_z(0, 0, last_lo)
         gather_gone(1, 0, S)
         make_unused(1, 0, S)
         make_left(1, 0, S)
         nc.vector.quantize_mx(
             out=w2_codes[:].bitcast(FP8X4), scales=w2_scales[:], in_=w2_grouped[:].rearrange("p c j -> p (c j)")
         )
-        make_z(1, 0, S)
+        make_z(1, 0, last_lo)
+        make_last_pair(0)
         pending = None
         for c in range(len(CHUNKS)):
             lo, hi = CHUNKS[c]
-            for step in (gather_use, gather_gone, make_unused, make_left, make_z):
+            for step in (gather_use, gather_gone, make_unused, make_left):
                 for t in (2, 3):
                     step(t, lo, hi)
                 if step is make_unused and pending is not None:
                     finish(c - 1, pending)
-            pending = interleave(c)
-        finish(len(CHUNKS) - 1, pending)
+            if lo < last_lo:
+                make_z(2, lo, hi)
+                make_z(3, lo, hi)
+                pending = interleave(c)
+        make_last_pair(2)
+        finish(len(CHUNKS) - 1, last_grouped)

@@ -42,14 +42,15 @@ def tile_picked_ystp_cur_p_kernel(tc, x_words, x_scales, w1, gap, base, rf, rd, 
         base_sb = per_row("base_sb", base, nc.gpsimd)
 
         gap_col = keep.tile([P, PACK], F32, name="gap_col")
-        nc.sync.dma_start(out=gap_col[:], in_=gap[0].rearrange("(p c) -> p c", c=PACK))
+        rf_sb = per_row("rf_sb", rf, nc.scalar)
+        rd_sb = per_row("rd_sb", rd, nc.scalar)
+        warm = keep.tile([P, 2], F32, name="warm")
+        nc.scalar.activation(warm[:, 0:1], identity[:, 0:1], ACT.Exp)
         for q in range(4):
-            nc.sync.dma_start(
+            nc.scalar.dma_start(
                 out=scale_window[32 * q : 32 * q + 4 * PASSES, :].bitcast(I32),
                 in_=x_scales[:, 4 * q : 4 * q + 4, :].bitcast(I32),
             )
-        rf_sb = per_row("rf_sb", rf, nc.scalar)
-        rd_sb = per_row("rd_sb", rd, nc.scalar)
 
         w1_raw = [keep.tile([P, PACK, H], F32, name=f"w1_raw{o}") for o in range(PASSES)]
         word_window = [keep.tile([P, T], U32, name=f"word_window{o}", align_bytes=64) for o in range(PASSES)]
@@ -59,9 +60,11 @@ def tile_picked_ystp_cur_p_kernel(tc, x_words, x_scales, w1, gap, base, rf, rd, 
         gone_rows = [keep.tile([P, U], F32, name=f"gone_rows{t}") for t in range(PACK)]
         w2_raw = keep.tile([P, PACK, N], F32, name="w2_raw")
 
-        for o in range(PASSES):
-            nc.sync.dma_start(out=w1_raw[o][:], in_=w1[512 * o : 512 * (o + 1), :].rearrange("(p j) c -> p j c", j=PACK))
+        w1_dealt = w1.rearrange("(o p j) c -> o p j c", p=P, j=PACK)
+        nc.sync.dma_start(out=gap_col[:], in_=gap[0].rearrange("(p c) -> p c", c=PACK))
+        nc.sync.dma_start(out=w1_raw[0][:], in_=w1_dealt[0])
         nc.sync.dma_start(offs_sb[:], offs)
+        nc.sync.dma_start(out=w1_raw[1][:], in_=w1_dealt[1])
         for o in range(PASSES):
             nc.sync.dma_start(
                 out=word_window[o][:].bitcast(I32),
@@ -79,22 +82,18 @@ def tile_picked_ystp_cur_p_kernel(tc, x_words, x_scales, w1, gap, base, rf, rd, 
         base_less_one = keep.tile([P, PACK], F32, name="base_less_one")
         nc.gpsimd.tensor_scalar(base_less_one[:], base_sb[:], 1.0, -1.0, ALU.mult, ALU.add)
 
-        fu = [keep.tile([P, S], F32, name=f"fu{t}") for t in range(PACK)]
-        fd = [keep.tile([P, S], F32, name=f"fd{t}") for t in range(PACK)]
-        fd_unit = [keep.tile([P, S], F32, name=f"fd_unit{t}") for t in range(PACK)]
-        gap_ps = psum.tile([P, PACK, P], F32, name="gap_ps")
+        gap_ps = psum.tile([P, PACK, P], F32, name="gap_ps", tag="spare")
         for c in range(PACK):
             nc.tensor.transpose(gap_ps[:, c, :], gap_col[:, c : c + 1].to_broadcast([P, P]), identity[:])
         gap_rows = gap_ps[:].rearrange("p c n -> p n c")
+        fu = [keep.tile([P, S], F32, name=f"fu{t}") for t in range(PACK)]
+        fd = [keep.tile([P, S], F32, name=f"fd{t}") for t in range(PACK)]
         for t in range(PACK):
-            nc.scalar.activation(
-                fu[t][:].rearrange("p (n c) -> p n c", c=PACK), gap_rows, ACT.Exp, scale=rf_sb[:, t : t + 1]
-            )
-            nc.scalar.activation(
-                fd[t][:].rearrange("p (n c) -> p n c", c=PACK), gap_rows, ACT.Exp, scale=rd_sb[:, t : t + 1]
-            )
-        for t in range(PACK):
-            nc.scalar.activation(fd_unit[t][:], fd[t][:], ACT.Copy, scale=unit_sb[:, t : t + 1])
+            for decay, rate in ((fu, rf_sb), (fd, rd_sb)):
+                nc.scalar.activation(
+                    decay[t][:].rearrange("p (n c) -> p n c", c=PACK), gap_rows, ACT.Exp, scale=rate[:, t : t + 1]
+                )
+        nc.scalar.activation(warm[:, 1:2], fd[PACK - 1][:, 0:1], ACT.Sigmoid)
 
         w1_codes = [keep.tile([P, H], U32, name=f"w1_codes{o}", align_bytes=64) for o in range(PASSES)]
         w1_scales = [keep.tile([P, H], U8, name=f"w1_scales{o}", align_bytes=64) for o in range(PASSES)]
@@ -126,6 +125,7 @@ def tile_picked_ystp_cur_p_kernel(tc, x_words, x_scales, w1, gap, base, rf, rd, 
                     stop=(o == PASSES - 1),
                 )
 
+        ss_unit = [keep.tile([P, S], F32, name=f"ss_unit{t}") for t in range(PACK)]
         ss = [keep.tile([P, S], F32, name=f"ss{t}") for t in range(PACK)]
         keepfrac = [keep.tile([P, S], F32, name=f"keepfrac{t}") for t in range(PACK)]
         for t in range(PACK):
@@ -133,6 +133,7 @@ def tile_picked_ystp_cur_p_kernel(tc, x_words, x_scales, w1, gap, base, rf, rd, 
             nc.scalar.activation(
                 keepfrac[t][:], ss[t][:], ACT.Copy, scale=base_sb[:, t : t + 1], bias=-1.0
             )
+            nc.scalar.activation(ss_unit[t][:], ss[t][:], ACT.Copy, scale=unit_sb[:, t : t + 1])
 
         w2_grouped = keep.tile([P, N, PACK], BF16, name="w2_grouped", align_bytes=64)
         w2_codes = keep.tile([P, N], U32, name="w2_codes", align_bytes=64)
@@ -142,71 +143,44 @@ def tile_picked_ystp_cur_p_kernel(tc, x_words, x_scales, w1, gap, base, rf, rd, 
             in_=w2_raw[:].rearrange("p j (c i) -> p c j i", i=4),
         )
 
-        a = [keep.tile([P, S], F32, name=f"a{t}") for t in range(PACK)]
-        g = [keep.tile([P, S], F32, name=f"g{t}") for t in range(PACK)]
+        a = keep.tile([P, PACK, S], F32, name="a")
+        g = keep.tile([P, PACK, S], F32, name="g")
         unused = keep.tile([P, PACK, S], F32, name="unused")
         left = keep.tile([P, PACK, S], F32, name="left")
-        z = keep.tile([P, PACK, CHUNKS[-1][0]], BF16, name="z")
+        z_low = keep.tile([P, 2, S], BF16, name="z_low")
+        z_grouped = keep.tile([P, S, PACK], BF16, name="z_grouped", align_bytes=64)
 
-        def gather_use(t, lo, hi):
-            picks = slot_sb[:, lo // LANES : hi // LANES]
-            nc.vector.tensor_tensor(a[t][:, lo:hi], use_rows[t][:].indirect(picks), fu[t][:, lo:hi], ALU.mult)
+        def gather_use(t):
+            nc.vector.tensor_tensor(a[:, t, :], use_rows[t][:].indirect(slot_sb[:]), fu[t][:], ALU.mult)
 
         def gather_gone(t, lo, hi):
             picks = slot_sb[:, lo // LANES : hi // LANES]
-            nc.vector.tensor_tensor(g[t][:, lo:hi], gone_rows[t][:].indirect(picks), fd_unit[t][:, lo:hi], ALU.mult)
+            nc.vector.tensor_tensor(g[:, t, lo:hi], gone_rows[t][:].indirect(picks), fd[t][:, lo:hi], ALU.mult)
 
-        def make_unused(t, lo, hi):
+        def make_unused(t):
             nc.vector.scalar_tensor_tensor(
-                unused[:, t, lo:hi], a[t][:, lo:hi], base_less_one[:, t : t + 1], keepfrac[t][:, lo:hi], ALU.add, ALU.mult
+                unused[:, t, :], a[:, t, :], base_less_one[:, t : t + 1], keepfrac[t][:], ALU.add, ALU.mult
             )
 
         def make_left(t, lo, hi):
             nc.vector.scalar_tensor_tensor(
-                left[:, t, lo:hi], g[t][:, lo:hi], unit_sb[:, t : t + 1], ss[t][:, lo:hi], ALU.subtract, ALU.mult
-            )
-
-        def make_z(t, lo, hi):
-            nc.vector.scalar_tensor_tensor(
-                z[:, t, lo:hi], unused[:, t, lo:hi], 1.0, left[:, t, lo:hi], ALU.subtract, ALU.mult
-            )
-
-        last_lo = CHUNKS[-1][0]
-        last_grouped = keep.tile([P, S - last_lo, PACK], BF16, name="last_grouped", align_bytes=64)
-
-        def make_last_pair(t):
-            nc.vector.scalar_tensor_tensor(
-                last_grouped[:, :, t : t + 2],
-                unused[:, t : t + 2, last_lo:].rearrange("p t j -> p j t"),
-                1.0,
-                left[:, t : t + 2, last_lo:].rearrange("p t j -> p j t"),
-                ALU.subtract,
-                ALU.mult,
+                left[:, t, lo:hi], g[:, t, lo:hi], 1.0, ss_unit[t][:, lo:hi], ALU.subtract, ALU.mult
             )
 
         out_dealt = out.rearrange("(m p) j -> p m j", p=P)
 
-        def interleave(c):
-            lo, hi = CHUNKS[c]
-            z_grouped = keep.tile([P, hi - lo, PACK], BF16, name=f"z_grouped{c}", align_bytes=64)
-            nc.scalar.copy(
-                out=z_grouped[:].rearrange("p (c i) t -> p c t i", i=4),
-                in_=z[:, :, lo:hi].rearrange("p t (c i) -> p c t i", i=4),
-            )
-            return z_grouped
-
-        def finish(c, z_grouped):
+        def finish(c):
             lo, hi = CHUNKS[c]
             z_codes = keep.tile([P, hi - lo], U32, name=f"z_codes{c}", align_bytes=64)
             z_scales = keep.tile([P, hi - lo], U8, name=f"z_scales{c}", align_bytes=64)
             nc.vector.quantize_mx(
-                out=z_codes[:].bitcast(FP8X4), scales=z_scales[:], in_=z_grouped[:].rearrange("p c t -> p (c t)")
+                out=z_codes[:].bitcast(FP8X4), scales=z_scales[:], in_=z_grouped[:, lo:hi, :].rearrange("p c t -> p (c t)")
             )
-            current = psum.tile([P, N // P, hi - lo], F32, name=f"current{c}")
-            for m in range(N // P):
+
+            def product(m, current):
                 cols = slice(P * m, P * (m + 1))
                 nc.tensor.matmul_mx(
-                    out=current[:, m, :],
+                    out=current,
                     lhsT=w2_codes[:, cols].bitcast(FP8X4),
                     lhsT_scale=w2_scales[:, cols],
                     rhs=z_codes[:].bitcast(FP8X4),
@@ -214,35 +188,50 @@ def tile_picked_ystp_cur_p_kernel(tc, x_words, x_scales, w1, gap, base, rf, rd, 
                     start=True,
                     stop=True,
                 )
-            result = keep.tile([P, N // P, hi - lo], F32, name=f"result{c}")
-            nc.scalar.copy(out=result[:], in_=current[:])
-            nc.sync.dma_start(out=out_dealt[:, :, lo:hi], in_=result[:])
 
-        gather_use(0, 0, S)
-        gather_gone(0, 0, S)
-        make_unused(0, 0, S)
-        make_left(0, 0, S)
-        gather_use(1, 0, S)
-        make_z(0, 0, last_lo)
-        gather_gone(1, 0, S)
-        make_unused(1, 0, S)
-        make_left(1, 0, S)
+            if c < len(CHUNKS) - 1:
+                current = psum.tile([P, 2, hi - lo], F32, name=f"current{c}")
+                product(0, current[:, 0, :])
+                product(1, current[:, 1, :])
+                result = keep.tile([P, 2, hi - lo], F32, name=f"result{c}")
+                nc.scalar.copy(out=result[:], in_=current[:])
+                nc.sync.dma_start(out=out_dealt[:, :, lo:hi], in_=result[:])
+            else:
+                upper = psum.tile([P, hi - lo], F32, name="upper")
+                lower = psum.tile([P, hi - lo], F32, name="lower", tag="spare")
+                product(0, upper[:])
+                product(1, lower[:])
+                upper_sb = keep.tile([P, hi - lo], F32, name="upper_sb")
+                lower_sb = keep.tile([P, hi - lo], F32, name="lower_sb")
+                nc.scalar.copy(out=upper_sb[:], in_=upper[:])
+                nc.scalar.dma_start(out=out_dealt[:, 0, lo:hi], in_=upper_sb[:])
+                nc.vector.tensor_copy(out=lower_sb[:], in_=lower[:])
+                nc.sync.dma_start(out=out_dealt[:, 1, lo:hi], in_=lower_sb[:])
+
+        for t in range(PACK - 1):
+            gather_use(t)
+            gather_gone(t, 0, S)
+            make_unused(t)
+            make_left(t, 0, S)
+            if t < 2:
+                nc.vector.scalar_tensor_tensor(
+                    z_low[:, t, :], unused[:, t, :], 1.0, left[:, t, :], ALU.subtract, ALU.mult
+                )
+        nc.scalar.copy(out=z_grouped[:, :, 0:2], in_=z_low[:].rearrange("p t j -> p j t"))
         nc.vector.quantize_mx(
             out=w2_codes[:].bitcast(FP8X4), scales=w2_scales[:], in_=w2_grouped[:].rearrange("p c j -> p (c j)")
         )
-        make_z(1, 0, last_lo)
-        make_last_pair(0)
-        pending = None
-        for c in range(len(CHUNKS)):
-            lo, hi = CHUNKS[c]
-            for step in (gather_use, gather_gone, make_unused, make_left):
-                for t in (2, 3):
-                    step(t, lo, hi)
-                if step is make_unused and pending is not None:
-                    finish(c - 1, pending)
-            if lo < last_lo:
-                make_z(2, lo, hi)
-                make_z(3, lo, hi)
-                pending = interleave(c)
-        make_last_pair(2)
-        finish(len(CHUNKS) - 1, last_grouped)
+        gather_use(PACK - 1)
+        make_unused(PACK - 1)
+        for c, (lo, hi) in enumerate(CHUNKS):
+            gather_gone(PACK - 1, lo, hi)
+            make_left(PACK - 1, lo, hi)
+            nc.vector.scalar_tensor_tensor(
+                z_grouped[:, lo:hi, 2:4],
+                unused[:, 2:4, lo:hi].rearrange("p t j -> p j t"),
+                1.0,
+                left[:, 2:4, lo:hi].rearrange("p t j -> p j t"),
+                ALU.subtract,
+                ALU.mult,
+            )
+            finish(c)

@@ -82,7 +82,7 @@ def tile_picked_ystp_cur_p_kernel(tc, x_words, x_scales, w1, gap, base, rf, rd, 
         base_less_one = keep.tile([P, PACK], F32, name="base_less_one")
         nc.gpsimd.tensor_scalar(base_less_one[:], base_sb[:], 1.0, -1.0, ALU.mult, ALU.add)
 
-        gap_ps = psum.tile([P, PACK, P], F32, name="gap_ps", tag="spare")
+        gap_ps = psum.tile([P, PACK, P], F32, name="gap_ps", tag="turned0")
         for c in range(PACK):
             nc.tensor.transpose(gap_ps[:, c, :], gap_col[:, c : c + 1].to_broadcast([P, P]), identity[:])
         gap_rows = gap_ps[:].rearrange("p c n -> p n c")
@@ -100,8 +100,8 @@ def tile_picked_ystp_cur_p_kernel(tc, x_words, x_scales, w1, gap, base, rf, rd, 
         w1_grouped = [keep.tile([P, H * PACK], BF16, name=f"w1_grouped{o}", align_bytes=64) for o in range(PASSES)]
         for o in range(PASSES):
             nc.vector.tensor_copy(
-                out=w1_grouped[o][:].rearrange("p (t m j) -> p m j t", t=PACK, j=PACK),
-                in_=w1_raw[o][:].rearrange("p j (m t) -> p m j t", t=PACK),
+                out=w1_grouped[o][:].rearrange("p (c i j) -> p c j i", i=4, j=PACK),
+                in_=w1_raw[o][:].rearrange("p j (c i) -> p c j i", i=4),
             )
             nc.vector.quantize_mx(out=w1_codes[o][:].bitcast(FP8X4), scales=w1_scales[o][:], in_=w1_grouped[o][:])
 
@@ -111,29 +111,31 @@ def tile_picked_ystp_cur_p_kernel(tc, x_words, x_scales, w1, gap, base, rf, rd, 
         for o in range(PASSES):
             nc.vector.tensor_copy(x_codes[o][:], word_window[o][:].indirect(offs_sb[:]))
 
-        drive = [psum.tile([P, S], F32, name=f"drive{t}") for t in range(PACK)]
+        drive = [psum.tile([P, H], F32, name=f"drive{n}", tag=f"product{n}") for n in range(S // P)]
         for o in range(PASSES):
-            for t in range(PACK):
-                cols = slice(P * t, P * (t + 1))
+            for n in range(S // P):
+                cols = slice(P * n, P * (n + 1))
                 nc.tensor.matmul_mx(
-                    out=drive[t][:],
-                    lhsT=w1_codes[o][:, cols].bitcast(FP8X4),
-                    lhsT_scale=w1_scales[o][:, cols],
-                    rhs=x_codes[o][:].bitcast(FP8X4),
-                    rhs_scale=x_scale[4 * o :, :],
+                    out=drive[n][:],
+                    lhsT=x_codes[o][:, cols].bitcast(FP8X4),
+                    lhsT_scale=x_scale[4 * o :, cols],
+                    rhs=w1_codes[o][:].bitcast(FP8X4),
+                    rhs_scale=w1_scales[o][:],
                     start=(o == 0),
                     stop=(o == PASSES - 1),
                 )
 
-        ss_unit = [keep.tile([P, S], F32, name=f"ss_unit{t}") for t in range(PACK)]
-        ss = [keep.tile([P, S], F32, name=f"ss{t}") for t in range(PACK)]
+        ss_rows = [keep.tile([P, PACK, P], F32, name=f"ss_rows{n}") for n in range(S // P)]
+        for n in range(S // P):
+            nc.scalar.activation(ss_rows[n][:], drive[n][:].rearrange("p (m t) -> p t m", t=PACK), ACT.Sigmoid)
         keepfrac = [keep.tile([P, S], F32, name=f"keepfrac{t}") for t in range(PACK)]
+        ss_unit = [keep.tile([P, S], F32, name=f"ss_unit{t}") for t in range(PACK)]
         for t in range(PACK):
-            nc.scalar.activation(ss[t][:], drive[t][:], ACT.Sigmoid)
-            nc.scalar.activation(
-                keepfrac[t][:], ss[t][:], ACT.Copy, scale=base_sb[:, t : t + 1], bias=-1.0
-            )
-            nc.scalar.activation(ss_unit[t][:], ss[t][:], ACT.Copy, scale=unit_sb[:, t : t + 1])
+            ss = psum.tile([P, S], F32, name=f"ss{t}", tag=f"turned{t}")
+            for n in range(S // P):
+                nc.tensor.transpose(ss[:, P * n : P * (n + 1)], ss_rows[n][:, t, :], identity[:])
+            nc.scalar.activation(keepfrac[t][:], ss[:], ACT.Copy, scale=base_sb[:, t : t + 1], bias=-1.0)
+            nc.scalar.activation(ss_unit[t][:], ss[:], ACT.Copy, scale=unit_sb[:, t : t + 1])
 
         w2_grouped = keep.tile([P, N, PACK], BF16, name="w2_grouped", align_bytes=64)
         w2_codes = keep.tile([P, N], U32, name="w2_codes", align_bytes=64)
@@ -190,15 +192,15 @@ def tile_picked_ystp_cur_p_kernel(tc, x_words, x_scales, w1, gap, base, rf, rd, 
                 )
 
             if c < len(CHUNKS) - 1:
-                current = psum.tile([P, 2, hi - lo], F32, name=f"current{c}")
+                current = psum.tile([P, 2, hi - lo], F32, name=f"current{c}", tag=f"product{c}")
                 product(0, current[:, 0, :])
                 product(1, current[:, 1, :])
                 result = keep.tile([P, 2, hi - lo], F32, name=f"result{c}")
                 nc.scalar.copy(out=result[:], in_=current[:])
                 nc.sync.dma_start(out=out_dealt[:, :, lo:hi], in_=result[:])
             else:
-                upper = psum.tile([P, hi - lo], F32, name="upper")
-                lower = psum.tile([P, hi - lo], F32, name="lower", tag="spare")
+                upper = psum.tile([P, hi - lo], F32, name="upper", tag="product2")
+                lower = psum.tile([P, hi - lo], F32, name="lower", tag="product3")
                 product(0, upper[:])
                 product(1, lower[:])
                 upper_sb = keep.tile([P, hi - lo], F32, name="upper_sb")

@@ -19,90 +19,99 @@ ALU = mybir.AluOpType
 P = 128
 PACK = 4
 PASSES = K // (P * PACK)
-LANES = 16
-CHUNKS = ((0, 256), (256, 384), (384, 512))
+QUADRANTS = 4
+SCALE_ROWS = 4
+LIST_ROWS = 16
+LINE = 4
+RANGES = ((0, 256), (256, 384), (384, 512))
 
 
-def tile_picked_ystp_cur_p_kernel(tc, x_words, x_scales, w1, gap, base, rf, rd, use, gone, w2, unit, offs, slot, out):
+def tile_picked_ystp_cur_p_kernel(
+    tc, x_words, x_scales, w1, gap, base, rf, rd, use, gone, w2, unit, offs, slot, out
+):
     nc = tc.nc
     with ExitStack() as ctx:
         keep = ctx.enter_context(tc.tile_pool(name="keep", bufs=1))
         psum = ctx.enter_context(tc.psum_pool(name="psum", bufs=1))
 
-        def per_row(name, vector, queue):
+        def load_by_plane(name, vector, queue):
             tile = keep.tile([P, PACK], F32, name=name)
             queue.dma_start(out=tile[:], in_=vector.rearrange("(p t) o -> p (t o)", t=PACK))
             return tile
 
+        def round_and_group(copy, grouped, raw):
+            copy(
+                out=grouped[:].rearrange("p (c i j) -> p c j i", i=LINE, j=PACK),
+                in_=raw[:].rearrange("p j (c i) -> p c j i", i=LINE),
+            )
+
         scale_window = keep.tile([P, T], U8, name="scale_window", align_bytes=64)
-        nc.vector.memset(scale_window[:].bitcast(I32), 0)
+        nc.gpsimd.memset(scale_window[:].bitcast(I32), 0)
         identity = keep.tile([P, P], F32, name="identity")
         make_identity(nc, identity[:])
-        unit_sb = per_row("unit_sb", unit, nc.gpsimd)
-        base_sb = per_row("base_sb", base, nc.gpsimd)
+        unit_sb = load_by_plane("unit_sb", unit, nc.gpsimd)
+        base_sb = load_by_plane("base_sb", base, nc.gpsimd)
 
         gap_col = keep.tile([P, PACK], F32, name="gap_col")
-        rf_sb = per_row("rf_sb", rf, nc.scalar)
-        rd_sb = per_row("rd_sb", rd, nc.scalar)
-        warm = keep.tile([P, 2], F32, name="warm")
-        nc.scalar.activation(warm[:, 0:1], identity[:, 0:1], ACT.Exp)
-        for q in range(4):
-            nc.scalar.dma_start(
-                out=scale_window[32 * q : 32 * q + 4 * PASSES, :].bitcast(I32),
-                in_=x_scales[:, 4 * q : 4 * q + 4, :].bitcast(I32),
-            )
+        nc.scalar.dma_start(out=gap_col[:], in_=gap[0].rearrange("(p c) -> p c", c=PACK))
+        rf_sb = load_by_plane("rf_sb", rf, nc.scalar)
+        rd_sb = load_by_plane("rd_sb", rd, nc.scalar)
 
         w1_raw = [keep.tile([P, PACK, H], F32, name=f"w1_raw{o}") for o in range(PASSES)]
         word_window = [keep.tile([P, T], U32, name=f"word_window{o}", align_bytes=64) for o in range(PASSES)]
-        offs_sb = keep.tile([P, S // LANES], U16, name="offs_sb")
-        slot_sb = keep.tile([P, S // LANES], U16, name="slot_sb")
+        offs_sb = keep.tile([P, S // LIST_ROWS], U16, name="offs_sb")
+        slot_sb = keep.tile([P, S // LIST_ROWS], U16, name="slot_sb")
         use_rows = [keep.tile([P, U], F32, name=f"use_rows{t}") for t in range(PACK)]
         gone_rows = [keep.tile([P, U], F32, name=f"gone_rows{t}") for t in range(PACK)]
         w2_raw = keep.tile([P, PACK, N], F32, name="w2_raw")
 
-        w1_dealt = w1.rearrange("(o p j) c -> o p j c", p=P, j=PACK)
-        nc.sync.dma_start(out=gap_col[:], in_=gap[0].rearrange("(p c) -> p c", c=PACK))
-        nc.sync.dma_start(out=w1_raw[0][:], in_=w1_dealt[0])
+        for q in range(QUADRANTS):
+            nc.sync.dma_start(
+                out=scale_window[32 * q : 32 * q + SCALE_ROWS * PASSES, :].bitcast(I32),
+                in_=x_scales[:, SCALE_ROWS * q : SCALE_ROWS * (q + 1), :].bitcast(I32),
+            )
         nc.sync.dma_start(offs_sb[:], offs)
-        nc.sync.dma_start(out=w1_raw[1][:], in_=w1_dealt[1])
+        w1_by_pass = w1.rearrange("(o p j) c -> o p j c", p=P, j=PACK)
+        for o in range(PASSES):
+            nc.sync.dma_start(out=w1_raw[o][:], in_=w1_by_pass[o])
         for o in range(PASSES):
             nc.sync.dma_start(
                 out=word_window[o][:].bitcast(I32),
                 in_=x_words[o].rearrange("p n t -> p (n t)").bitcast(I32),
             )
         nc.sync.dma_start(slot_sb[:], slot)
-        use_dealt = use.rearrange("(p t) u -> t p u", t=PACK)
-        gone_dealt = gone.rearrange("(p t) u -> t p u", t=PACK)
+        use_by_plane = use.rearrange("(p t) u -> t p u", t=PACK)
+        gone_by_plane = gone.rearrange("(p t) u -> t p u", t=PACK)
+        table_loads = []
         for t in range(PACK):
-            nc.sync.dma_start(out=use_rows[t][:], in_=use_dealt[t])
-            nc.sync.dma_start(out=gone_rows[t][:], in_=gone_dealt[t])
-            if t == 1:
-                nc.sync.dma_start(out=w2_raw[:], in_=w2.rearrange("(p j) c -> p j c", j=PACK))
+            table_loads.append((use_rows[t], use_by_plane[t]))
+            table_loads.append((gone_rows[t], gone_by_plane[t]))
+        for tile, rows in table_loads[:-3]:
+            nc.sync.dma_start(out=tile[:], in_=rows)
+        nc.sync.dma_start(out=w2_raw[:], in_=w2.rearrange("(p j) c -> p j c", j=PACK))
+        for tile, rows in table_loads[-3:]:
+            nc.sync.dma_start(out=tile[:], in_=rows)
 
         base_less_one = keep.tile([P, PACK], F32, name="base_less_one")
-        nc.gpsimd.tensor_scalar(base_less_one[:], base_sb[:], 1.0, -1.0, ALU.mult, ALU.add)
+        nc.scalar.activation(base_less_one[:], base_sb[:], ACT.Copy, bias=-1.0)
 
-        gap_ps = psum.tile([P, PACK, P], F32, name="gap_ps", tag="turned0")
+        gap_spread = psum.tile([P, PACK, P], F32, name="gap_spread", tag="turned0")
         for c in range(PACK):
-            nc.tensor.transpose(gap_ps[:, c, :], gap_col[:, c : c + 1].to_broadcast([P, P]), identity[:])
-        gap_rows = gap_ps[:].rearrange("p c n -> p n c")
+            nc.tensor.transpose(gap_spread[:, c, :], gap_col[:, c : c + 1].to_broadcast([P, P]), identity[:])
+        gap_in_order = gap_spread[:].rearrange("p c n -> p n c")
         fu = [keep.tile([P, S], F32, name=f"fu{t}") for t in range(PACK)]
         fd = [keep.tile([P, S], F32, name=f"fd{t}") for t in range(PACK)]
         for t in range(PACK):
             for decay, rate in ((fu, rf_sb), (fd, rd_sb)):
                 nc.scalar.activation(
-                    decay[t][:].rearrange("p (n c) -> p n c", c=PACK), gap_rows, ACT.Exp, scale=rate[:, t : t + 1]
+                    decay[t][:].rearrange("p (n c) -> p n c", c=PACK), gap_in_order, ACT.Exp, scale=rate[:, t : t + 1]
                 )
-        nc.scalar.activation(warm[:, 1:2], fd[PACK - 1][:, 0:1], ACT.Sigmoid)
 
         w1_codes = [keep.tile([P, H], U32, name=f"w1_codes{o}", align_bytes=64) for o in range(PASSES)]
         w1_scales = [keep.tile([P, H], U8, name=f"w1_scales{o}", align_bytes=64) for o in range(PASSES)]
         w1_grouped = [keep.tile([P, H * PACK], BF16, name=f"w1_grouped{o}", align_bytes=64) for o in range(PASSES)]
         for o in range(PASSES):
-            nc.vector.tensor_copy(
-                out=w1_grouped[o][:].rearrange("p (c i j) -> p c j i", i=4, j=PACK),
-                in_=w1_raw[o][:].rearrange("p j (c i) -> p c j i", i=4),
-            )
+            round_and_group(nc.vector.tensor_copy, w1_grouped[o], w1_raw[o])
             nc.vector.quantize_mx(out=w1_codes[o][:].bitcast(FP8X4), scales=w1_scales[o][:], in_=w1_grouped[o][:])
 
         x_scale = keep.tile([P, S], U8, name="x_scale", align_bytes=64)
@@ -114,11 +123,11 @@ def tile_picked_ystp_cur_p_kernel(tc, x_words, x_scales, w1, gap, base, rf, rd, 
         drive = [psum.tile([P, H], F32, name=f"drive{n}", tag=f"product{n}") for n in range(S // P)]
         for o in range(PASSES):
             for n in range(S // P):
-                cols = slice(P * n, P * (n + 1))
+                networks = slice(P * n, P * (n + 1))
                 nc.tensor.matmul_mx(
                     out=drive[n][:],
-                    lhsT=x_codes[o][:, cols].bitcast(FP8X4),
-                    lhsT_scale=x_scale[4 * o :, cols],
+                    lhsT=x_codes[o][:, networks].bitcast(FP8X4),
+                    lhsT_scale=x_scale[SCALE_ROWS * o :, networks],
                     rhs=w1_codes[o][:].bitcast(FP8X4),
                     rhs_scale=w1_scales[o][:],
                     start=(o == 0),
@@ -128,22 +137,19 @@ def tile_picked_ystp_cur_p_kernel(tc, x_words, x_scales, w1, gap, base, rf, rd, 
         ss_rows = [keep.tile([P, PACK, P], F32, name=f"ss_rows{n}") for n in range(S // P)]
         for n in range(S // P):
             nc.scalar.activation(ss_rows[n][:], drive[n][:].rearrange("p (m t) -> p t m", t=PACK), ACT.Sigmoid)
-        keepfrac = [keep.tile([P, S], F32, name=f"keepfrac{t}") for t in range(PACK)]
-        ss_unit = [keep.tile([P, S], F32, name=f"ss_unit{t}") for t in range(PACK)]
+        base_ss_less_one = [keep.tile([P, S], F32, name=f"base_ss_less_one{t}") for t in range(PACK)]
+        unit_ss = [keep.tile([P, S], F32, name=f"unit_ss{t}") for t in range(PACK)]
         for t in range(PACK):
             ss = psum.tile([P, S], F32, name=f"ss{t}", tag=f"turned{t}")
             for n in range(S // P):
                 nc.tensor.transpose(ss[:, P * n : P * (n + 1)], ss_rows[n][:, t, :], identity[:])
-            nc.scalar.activation(keepfrac[t][:], ss[:], ACT.Copy, scale=base_sb[:, t : t + 1], bias=-1.0)
-            nc.scalar.activation(ss_unit[t][:], ss[:], ACT.Copy, scale=unit_sb[:, t : t + 1])
+            nc.scalar.activation(base_ss_less_one[t][:], ss[:], ACT.Copy, scale=base_sb[:, t : t + 1], bias=-1.0)
+            nc.scalar.activation(unit_ss[t][:], ss[:], ACT.Copy, scale=unit_sb[:, t : t + 1])
 
-        w2_grouped = keep.tile([P, N, PACK], BF16, name="w2_grouped", align_bytes=64)
+        w2_grouped = keep.tile([P, N * PACK], BF16, name="w2_grouped", align_bytes=64)
         w2_codes = keep.tile([P, N], U32, name="w2_codes", align_bytes=64)
         w2_scales = keep.tile([P, N], U8, name="w2_scales", align_bytes=64)
-        nc.scalar.copy(
-            out=w2_grouped[:].rearrange("p (c i) j -> p c j i", i=4),
-            in_=w2_raw[:].rearrange("p j (c i) -> p c j i", i=4),
-        )
+        round_and_group(nc.scalar.copy, w2_grouped, w2_raw)
 
         a = keep.tile([P, PACK, S], F32, name="a")
         g = keep.tile([P, PACK, S], F32, name="g")
@@ -156,61 +162,64 @@ def tile_picked_ystp_cur_p_kernel(tc, x_words, x_scales, w1, gap, base, rf, rd, 
             nc.vector.tensor_tensor(a[:, t, :], use_rows[t][:].indirect(slot_sb[:]), fu[t][:], ALU.mult)
 
         def gather_gone(t, lo, hi):
-            picks = slot_sb[:, lo // LANES : hi // LANES]
+            picks = slot_sb[:, lo // LIST_ROWS : hi // LIST_ROWS]
             nc.vector.tensor_tensor(g[:, t, lo:hi], gone_rows[t][:].indirect(picks), fd[t][:, lo:hi], ALU.mult)
 
         def make_unused(t):
             nc.vector.scalar_tensor_tensor(
-                unused[:, t, :], a[:, t, :], base_less_one[:, t : t + 1], keepfrac[t][:], ALU.add, ALU.mult
+                unused[:, t, :], a[:, t, :], base_less_one[:, t : t + 1], base_ss_less_one[t][:], ALU.add, ALU.mult
             )
 
         def make_left(t, lo, hi):
             nc.vector.scalar_tensor_tensor(
-                left[:, t, lo:hi], g[:, t, lo:hi], 1.0, ss_unit[t][:, lo:hi], ALU.subtract, ALU.mult
+                left[:, t, lo:hi], g[:, t, lo:hi], 1.0, unit_ss[t][:, lo:hi], ALU.subtract, ALU.mult
             )
 
-        out_dealt = out.rearrange("(m p) j -> p m j", p=P)
+        out_by_half = out.rearrange("(m p) j -> p m j", p=P)
 
-        def finish(c):
-            lo, hi = CHUNKS[c]
+        def second_product(c):
+            lo, hi = RANGES[c]
             z_codes = keep.tile([P, hi - lo], U32, name=f"z_codes{c}", align_bytes=64)
             z_scales = keep.tile([P, hi - lo], U8, name=f"z_scales{c}", align_bytes=64)
             nc.vector.quantize_mx(
-                out=z_codes[:].bitcast(FP8X4), scales=z_scales[:], in_=z_grouped[:, lo:hi, :].rearrange("p c t -> p (c t)")
+                out=z_codes[:].bitcast(FP8X4),
+                scales=z_scales[:],
+                in_=z_grouped[:, lo:hi, :].rearrange("p j t -> p (j t)"),
             )
 
-            def product(m, current):
-                cols = slice(P * m, P * (m + 1))
+            def multiply(m, bank):
+                cells = slice(P * m, P * (m + 1))
                 nc.tensor.matmul_mx(
-                    out=current,
-                    lhsT=w2_codes[:, cols].bitcast(FP8X4),
-                    lhsT_scale=w2_scales[:, cols],
+                    out=bank,
+                    lhsT=w2_codes[:, cells].bitcast(FP8X4),
+                    lhsT_scale=w2_scales[:, cells],
                     rhs=z_codes[:].bitcast(FP8X4),
                     rhs_scale=z_scales[:],
                     start=True,
                     stop=True,
                 )
 
-            if c < len(CHUNKS) - 1:
+            if c < len(RANGES) - 1:
                 current = psum.tile([P, 2, hi - lo], F32, name=f"current{c}", tag=f"product{c}")
-                product(0, current[:, 0, :])
-                product(1, current[:, 1, :])
+                multiply(0, current[:, 0, :])
+                multiply(1, current[:, 1, :])
                 result = keep.tile([P, 2, hi - lo], F32, name=f"result{c}")
                 nc.scalar.copy(out=result[:], in_=current[:])
-                nc.sync.dma_start(out=out_dealt[:, :, lo:hi], in_=result[:])
+                nc.sync.dma_start(out=out_by_half[:, :, lo:hi], in_=result[:])
             else:
                 upper = psum.tile([P, hi - lo], F32, name="upper", tag="product2")
                 lower = psum.tile([P, hi - lo], F32, name="lower", tag="product3")
-                product(0, upper[:])
-                product(1, lower[:])
+                multiply(0, upper[:])
+                multiply(1, lower[:])
                 upper_sb = keep.tile([P, hi - lo], F32, name="upper_sb")
                 lower_sb = keep.tile([P, hi - lo], F32, name="lower_sb")
                 nc.scalar.copy(out=upper_sb[:], in_=upper[:])
-                nc.scalar.dma_start(out=out_dealt[:, 0, lo:hi], in_=upper_sb[:])
+                nc.scalar.dma_start(out=out_by_half[:, 0, lo:hi], in_=upper_sb[:])
                 nc.vector.tensor_copy(out=lower_sb[:], in_=lower[:])
-                nc.sync.dma_start(out=out_dealt[:, 1, lo:hi], in_=lower_sb[:])
+                nc.sync.dma_start(out=out_by_half[:, 1, lo:hi], in_=lower_sb[:])
 
-        for t in range(PACK - 1):
+        last = PACK - 1
+        for t in range(last):
             gather_use(t)
             gather_gone(t, 0, S)
             make_unused(t)
@@ -220,14 +229,12 @@ def tile_picked_ystp_cur_p_kernel(tc, x_words, x_scales, w1, gap, base, rf, rd, 
                     z_low[:, t, :], unused[:, t, :], 1.0, left[:, t, :], ALU.subtract, ALU.mult
                 )
         nc.scalar.copy(out=z_grouped[:, :, 0:2], in_=z_low[:].rearrange("p t j -> p j t"))
-        nc.vector.quantize_mx(
-            out=w2_codes[:].bitcast(FP8X4), scales=w2_scales[:], in_=w2_grouped[:].rearrange("p c j -> p (c j)")
-        )
-        gather_use(PACK - 1)
-        make_unused(PACK - 1)
-        for c, (lo, hi) in enumerate(CHUNKS):
-            gather_gone(PACK - 1, lo, hi)
-            make_left(PACK - 1, lo, hi)
+        nc.vector.quantize_mx(out=w2_codes[:].bitcast(FP8X4), scales=w2_scales[:], in_=w2_grouped[:])
+        gather_use(last)
+        make_unused(last)
+        for c, (lo, hi) in enumerate(RANGES):
+            gather_gone(last, lo, hi)
+            make_left(last, lo, hi)
             nc.vector.scalar_tensor_tensor(
                 z_grouped[:, lo:hi, 2:4],
                 unused[:, 2:4, lo:hi].rearrange("p t j -> p j t"),
@@ -236,4 +243,4 @@ def tile_picked_ystp_cur_p_kernel(tc, x_words, x_scales, w1, gap, base, rf, rd, 
                 ALU.subtract,
                 ALU.mult,
             )
-            finish(c)
+            second_product(c)

from contextlib import ExitStack

import concourse.mybir as mybir
from concourse.masks import make_identity

K, T, S, H, N, U = 1024, 2048, 512, 512, 256, 1024
FLOPS = 2 * K * H * S + 2 * H * N * S

F32 = mybir.dt.float32
BF16 = mybir.dt.bfloat16
I32 = mybir.dt.int32
U32 = mybir.dt.uint32
U16 = mybir.dt.uint16
U8 = mybir.dt.uint8
FP8X4 = mybir.dt.float8_e4m3fn_x4
ACT = mybir.ActivationFunctionType
ALU = mybir.AluOpType

P = 128
PACK = 4
PASSES = K // (P * PACK)
QUADRANTS = 4
SCALE_ROWS = 4
LIST_ROWS = 16
LINE = 4
RANGES = ((0, 256), (256, 384), (384, 512))


def tile_picked_ystp_cur_p_kernel(
    tc, x_words, x_scales, w1, gap, base, rf, rd, use, gone, w2, unit, offs, slot, out
):
    nc = tc.nc
    with ExitStack() as ctx:
        keep = ctx.enter_context(tc.tile_pool(name="keep", bufs=1))
        psum = ctx.enter_context(tc.psum_pool(name="psum", bufs=1))

        def load_by_plane(name, vector, queue):
            tile = keep.tile([P, PACK], F32, name=name)
            queue.dma_start(out=tile[:], in_=vector.rearrange("(p t) o -> p (t o)", t=PACK))
            return tile

        def round_and_group(copy, grouped, raw):
            copy(
                out=grouped[:].rearrange("p (c i j) -> p c j i", i=LINE, j=PACK),
                in_=raw[:].rearrange("p j (c i) -> p c j i", i=LINE),
            )

        scale_window = keep.tile([P, T], U8, name="scale_window", align_bytes=64)
        nc.gpsimd.memset(scale_window[:].bitcast(I32), 0)
        identity = keep.tile([P, P], F32, name="identity")
        make_identity(nc, identity[:])
        unit_sb = load_by_plane("unit_sb", unit, nc.gpsimd)
        base_sb = load_by_plane("base_sb", base, nc.gpsimd)

        gap_col = keep.tile([P, PACK], F32, name="gap_col")
        nc.scalar.dma_start(out=gap_col[:], in_=gap[0].rearrange("(p c) -> p c", c=PACK))
        rf_sb = load_by_plane("rf_sb", rf, nc.scalar)
        rd_sb = load_by_plane("rd_sb", rd, nc.scalar)

        w1_raw = [keep.tile([P, PACK, H], F32, name=f"w1_raw{o}") for o in range(PASSES)]
        word_window = [keep.tile([P, T], U32, name=f"word_window{o}", align_bytes=64) for o in range(PASSES)]
        offs_sb = keep.tile([P, S // LIST_ROWS], U16, name="offs_sb")
        slot_sb = keep.tile([P, S // LIST_ROWS], U16, name="slot_sb")
        use_rows = [keep.tile([P, U], F32, name=f"use_rows{t}") for t in range(PACK)]
        gone_rows = [keep.tile([P, U], F32, name=f"gone_rows{t}") for t in range(PACK)]
        w2_raw = keep.tile([P, PACK, N], F32, name="w2_raw")

        for q in range(QUADRANTS):
            nc.sync.dma_start(
                out=scale_window[32 * q : 32 * q + SCALE_ROWS * PASSES, :].bitcast(I32),
                in_=x_scales[:, SCALE_ROWS * q : SCALE_ROWS * (q + 1), :].bitcast(I32),
            )
        nc.sync.dma_start(offs_sb[:], offs)
        w1_by_pass = w1.rearrange("(o p j) c -> o p j c", p=P, j=PACK)
        for o in range(PASSES):
            nc.sync.dma_start(out=w1_raw[o][:], in_=w1_by_pass[o])
        for o in range(PASSES):
            nc.sync.dma_start(
                out=word_window[o][:].bitcast(I32),
                in_=x_words[o].rearrange("p n t -> p (n t)").bitcast(I32),
            )
        nc.sync.dma_start(slot_sb[:], slot)
        use_by_plane = use.rearrange("(p t) u -> t p u", t=PACK)
        gone_by_plane = gone.rearrange("(p t) u -> t p u", t=PACK)
        table_loads = []
        for t in range(PACK):
            table_loads.append((use_rows[t], use_by_plane[t]))
            table_loads.append((gone_rows[t], gone_by_plane[t]))
        for tile, rows in table_loads[:-3]:
            nc.sync.dma_start(out=tile[:], in_=rows)
        nc.sync.dma_start(out=w2_raw[:], in_=w2.rearrange("(p j) c -> p j c", j=PACK))
        for tile, rows in table_loads[-3:]:
            nc.sync.dma_start(out=tile[:], in_=rows)

        base_less_one = keep.tile([P, PACK], F32, name="base_less_one")
        nc.scalar.activation(base_less_one[:], base_sb[:], ACT.Copy, bias=-1.0)

        gap_spread = psum.tile([P, PACK, P], F32, name="gap_spread", tag="turned0")
        for c in range(PACK):
            nc.tensor.transpose(gap_spread[:, c, :], gap_col[:, c : c + 1].to_broadcast([P, P]), identity[:])
        gap_in_order = gap_spread[:].rearrange("p c n -> p n c")
        fu = [keep.tile([P, S], F32, name=f"fu{t}") for t in range(PACK)]
        fd = [keep.tile([P, S], F32, name=f"fd{t}") for t in range(PACK)]
        for t in range(PACK):
            for decay, rate in ((fu, rf_sb), (fd, rd_sb)):
                nc.scalar.activation(
                    decay[t][:].rearrange("p (n c) -> p n c", c=PACK), gap_in_order, ACT.Exp, scale=rate[:, t : t + 1]
                )

        w1_codes = [keep.tile([P, H], U32, name=f"w1_codes{o}", align_bytes=64) for o in range(PASSES)]
        w1_scales = [keep.tile([P, H], U8, name=f"w1_scales{o}", align_bytes=64) for o in range(PASSES)]
        w1_grouped = [keep.tile([P, H * PACK], BF16, name=f"w1_grouped{o}", align_bytes=64) for o in range(PASSES)]
        for o in range(PASSES):
            round_and_group(nc.vector.tensor_copy, w1_grouped[o], w1_raw[o])
            nc.vector.quantize_mx(out=w1_codes[o][:].bitcast(FP8X4), scales=w1_scales[o][:], in_=w1_grouped[o][:])

        x_scale = keep.tile([P, S], U8, name="x_scale", align_bytes=64)
        nc.vector.tensor_copy(x_scale[:], scale_window[:].indirect(offs_sb[:]))
        x_codes = [keep.tile([P, S], U32, name=f"x_codes{o}", align_bytes=64) for o in range(PASSES)]
        for o in range(PASSES):
            nc.vector.tensor_copy(x_codes[o][:], word_window[o][:].indirect(offs_sb[:]))

        drive = [psum.tile([P, H], F32, name=f"drive{n}", tag=f"product{n}") for n in range(S // P)]
        for o in range(PASSES):
            for n in range(S // P):
                networks = slice(P * n, P * (n + 1))
                nc.tensor.matmul_mx(
                    out=drive[n][:],
                    lhsT=x_codes[o][:, networks].bitcast(FP8X4),
                    lhsT_scale=x_scale[SCALE_ROWS * o :, networks],
                    rhs=w1_codes[o][:].bitcast(FP8X4),
                    rhs_scale=w1_scales[o][:],
                    start=(o == 0),
                    stop=(o == PASSES - 1),
                )

        ss_rows = [keep.tile([P, PACK, P], F32, name=f"ss_rows{n}") for n in range(S // P)]
        for n in range(S // P):
            nc.scalar.activation(ss_rows[n][:], drive[n][:].rearrange("p (m t) -> p t m", t=PACK), ACT.Sigmoid)
        base_ss_less_one = [keep.tile([P, S], F32, name=f"base_ss_less_one{t}") for t in range(PACK)]
        unit_ss = [keep.tile([P, S], F32, name=f"unit_ss{t}") for t in range(PACK)]
        for t in range(PACK):
            ss = psum.tile([P, S], F32, name=f"ss{t}", tag=f"turned{t}")
            for n in range(S // P):
                nc.tensor.transpose(ss[:, P * n : P * (n + 1)], ss_rows[n][:, t, :], identity[:])
            nc.scalar.activation(base_ss_less_one[t][:], ss[:], ACT.Copy, scale=base_sb[:, t : t + 1], bias=-1.0)
            nc.scalar.activation(unit_ss[t][:], ss[:], ACT.Copy, scale=unit_sb[:, t : t + 1])

        w2_grouped = keep.tile([P, N * PACK], BF16, name="w2_grouped", align_bytes=64)
        w2_codes = keep.tile([P, N], U32, name="w2_codes", align_bytes=64)
        w2_scales = keep.tile([P, N], U8, name="w2_scales", align_bytes=64)
        round_and_group(nc.scalar.copy, w2_grouped, w2_raw)

        a = keep.tile([P, PACK, S], F32, name="a")
        g = keep.tile([P, PACK, S], F32, name="g")
        unused = keep.tile([P, PACK, S], F32, name="unused")
        left = keep.tile([P, PACK, S], F32, name="left")
        z_low = keep.tile([P, 2, S], BF16, name="z_low")
        z_grouped = keep.tile([P, S, PACK], BF16, name="z_grouped", align_bytes=64)

        def gather_use(t):
            nc.vector.tensor_tensor(a[:, t, :], use_rows[t][:].indirect(slot_sb[:]), fu[t][:], ALU.mult)

        def gather_gone(t, lo, hi):
            picks = slot_sb[:, lo // LIST_ROWS : hi // LIST_ROWS]
            nc.vector.tensor_tensor(g[:, t, lo:hi], gone_rows[t][:].indirect(picks), fd[t][:, lo:hi], ALU.mult)

        def make_unused(t):
            nc.vector.scalar_tensor_tensor(
                unused[:, t, :], a[:, t, :], base_less_one[:, t : t + 1], base_ss_less_one[t][:], ALU.add, ALU.mult
            )

        def make_left(t, lo, hi):
            nc.vector.scalar_tensor_tensor(
                left[:, t, lo:hi], g[:, t, lo:hi], 1.0, unit_ss[t][:, lo:hi], ALU.subtract, ALU.mult
            )

        out_by_half = out.rearrange("(m p) j -> p m j", p=P)

        def second_product(c):
            lo, hi = RANGES[c]
            z_codes = keep.tile([P, hi - lo], U32, name=f"z_codes{c}", align_bytes=64)
            z_scales = keep.tile([P, hi - lo], U8, name=f"z_scales{c}", align_bytes=64)
            nc.vector.quantize_mx(
                out=z_codes[:].bitcast(FP8X4),
                scales=z_scales[:],
                in_=z_grouped[:, lo:hi, :].rearrange("p j t -> p (j t)"),
            )

            def multiply(m, bank):
                cells = slice(P * m, P * (m + 1))
                nc.tensor.matmul_mx(
                    out=bank,
                    lhsT=w2_codes[:, cells].bitcast(FP8X4),
                    lhsT_scale=w2_scales[:, cells],
                    rhs=z_codes[:].bitcast(FP8X4),
                    rhs_scale=z_scales[:],
                    start=True,
                    stop=True,
                )

            if c < len(RANGES) - 1:
                current = psum.tile([P, 2, hi - lo], F32, name=f"current{c}", tag=f"product{c}")
                multiply(0, current[:, 0, :])
                multiply(1, current[:, 1, :])
                result = keep.tile([P, 2, hi - lo], F32, name=f"result{c}")
                nc.scalar.copy(out=result[:], in_=current[:])
                nc.sync.dma_start(out=out_by_half[:, :, lo:hi], in_=result[:])
            else:
                upper = psum.tile([P, hi - lo], F32, name="upper", tag="product2")
                lower = psum.tile([P, hi - lo], F32, name="lower", tag="product3")
                multiply(0, upper[:])
                multiply(1, lower[:])
                upper_sb = keep.tile([P, hi - lo], F32, name="upper_sb")
                lower_sb = keep.tile([P, hi - lo], F32, name="lower_sb")
                nc.scalar.copy(out=upper_sb[:], in_=upper[:])
                nc.scalar.dma_start(out=out_by_half[:, 0, lo:hi], in_=upper_sb[:])
                nc.vector.tensor_copy(out=lower_sb[:], in_=lower[:])
                nc.sync.dma_start(out=out_by_half[:, 1, lo:hi], in_=lower_sb[:])

        last = PACK - 1
        for t in range(last):
            gather_use(t)
            gather_gone(t, 0, S)
            make_unused(t)
            make_left(t, 0, S)
            if t < 2:
                nc.vector.scalar_tensor_tensor(
                    z_low[:, t, :], unused[:, t, :], 1.0, left[:, t, :], ALU.subtract, ALU.mult
                )
        nc.scalar.copy(out=z_grouped[:, :, 0:2], in_=z_low[:].rearrange("p t j -> p j t"))
        nc.vector.quantize_mx(out=w2_codes[:].bitcast(FP8X4), scales=w2_scales[:], in_=w2_grouped[:])
        gather_use(last)
        make_unused(last)
        for c, (lo, hi) in enumerate(RANGES):
            gather_gone(last, lo, hi)
            make_left(last, lo, hi)
            nc.vector.scalar_tensor_tensor(
                z_grouped[:, lo:hi, 2:4],
                unused[:, 2:4, lo:hi].rearrange("p t j -> p j t"),
                1.0,
                left[:, 2:4, lo:hi].rearrange("p t j -> p j t"),
                ALU.subtract,
                ALU.mult,
            )
            second_product(c)
